import numpy as np
import ml_dtypes


def mxq(x, axis, fmt="e4m3"):
    dtype, down = {"e4m3": (ml_dtypes.float8_e4m3fn, 7), "e5m2": (ml_dtypes.float8_e5m2, 14)}[fmt]
    v = np.moveaxis(np.asarray(x, np.float32).astype(ml_dtypes.bfloat16).astype(np.float64), axis, -1)
    blocks = v.reshape(v.shape[:-1] + (-1, 32))
    amax = np.abs(blocks).max(-1, keepdims=True)
    byte = np.maximum(np.where(amax > 0, np.frexp(amax)[1] - 1 + 127, 0) - down, 1)
    scale = np.exp2(byte - 127.0)
    codes = (blocks / scale).astype(np.float32).astype(dtype).astype(np.float64)
    return np.moveaxis((codes * scale).reshape(v.shape), -1, axis)


WIDE = False


def mx_kscale(k):
    if not WIDE:
        return np.ones(k)
    levels = np.array([10, -10, 5, -5, 0])
    if k % 512:
        return np.exp2(np.random.permutation(np.resize(levels, k // 32))).repeat(32)
    a = np.empty((k // 512, 16))
    for p in range(k // 512):
        a[p, :8] = np.random.permutation(np.resize(levels, 8))
        for g in range(8):
            far = levels[np.abs(levels - a[p, g]) >= 10]
            a[p, g + 8] = far[np.random.randint(len(far))]
    return np.exp2(a.ravel()).repeat(32)


def f64(x):
    return np.asarray(x).astype(np.float64)


def striped8(idx):
    return np.asarray(idx).reshape(8, -1, 16).transpose(0, 2, 1).reshape(128, -1).astype(np.uint16)


def unstriped8(offs):
    return offs.reshape(8, 16, -1).transpose(0, 2, 1).reshape(8, -1).astype(np.int64)


def pick8(x, idx, run):
    r = np.arange(len(x))
    return x[r[:, None], idx[r % (8 * run) // run]]


E2M1 = np.array([0.0, 0.5, 1.0, 1.5, 2.0, 3.0, 4.0, 6.0, -0.0, -0.5, -1.0, -1.5, -2.0, -3.0, -4.0, -6.0])


def pack_weight(w, fmt):
    k, n = w.shape
    w = f64(np.asarray(w, np.float32).astype(ml_dtypes.bfloat16)).reshape(k // 32, 32, n)
    amax = np.abs(w).max(1)
    if fmt == "e4m3":
        byte = np.frexp(amax)[1] - 1 + 127 - 7
    else:
        mant, ex = np.frexp(amax / 6.0)
        byte = np.where(mant > 0.5, ex, ex - 1) + 127
    byte = np.clip(np.where(amax > 0, byte, 1), 1, 254)
    scaled = (w * np.exp2(127.0 - byte)[:, None, :]).reshape(k, n).astype(np.float32)
    by_word = np.ascontiguousarray(scaled.reshape(k // 512, 128, 4, n).transpose(0, 1, 3, 2))
    if fmt == "e4m3":
        words = by_word.astype(ml_dtypes.float8_e4m3fn).view(np.uint8)
    else:
        c = by_word.astype(ml_dtypes.float4_e2m1fn).view(np.uint8) & 0xF
        words = (c[..., 0::2] | (c[..., 1::2] << 4)).reshape(k // 512, 128, 2 * n)
    return np.ascontiguousarray(words), np.ascontiguousarray(byte.astype(np.uint8).reshape(k // 512, 16, n))


def unpack_weight(words, scales, fmt):
    g, _, n = scales.shape
    words = np.ascontiguousarray(words).reshape(g, 128, n, -1)
    if fmt == "e4m3":
        vals = words.view(ml_dtypes.float8_e4m3fn).astype(np.float64)
    else:
        nib = np.empty((g, 128, n, 4), np.uint8)
        nib[..., 0::2] = words & 0xF
        nib[..., 1::2] = words >> 4
        vals = E2M1[nib]
    vals = vals * np.repeat(np.exp2(scales.astype(np.float64) - 127.0), 8, axis=1)[..., None]
    return vals.transpose(0, 1, 3, 2).reshape(g * 512, n)


D, V, Q, I = 512, 2048, 128, 512


def setup_inputs():
    n = np.random.standard_normal
    idx = np.stack([np.random.permutation(V)[:I] for _ in range(8)])
    fd = mx_kscale(D)
    vocp = pack_weight(n((D, V)) / fd[:, None], "e2m1")
    return {
        "hid": (n((D, Q)) * 1.0 / np.sqrt(D) * fd[:, None]).astype(np.float32),
        "voc_words": vocp[0],
        "voc_scales": vocp[1],
        "aim": (np.random.uniform(0.1, 0.6, (Q, 1))).astype(np.float32),
        "cw1": (np.random.uniform(0.5, 1.5, (1, I))).astype(np.float32),
        "sw": (np.random.uniform(20.0, 80.0, (1, I))).astype(np.float32),
        "dhid": (n((D, Q)) * 1.0 / np.sqrt(D) * fd[:, None]).astype(np.float32),
        "base": (0.5 * n((Q, V))).astype(np.float32),
        "offs": striped8(idx),
    }


def reference(hid, voc_words, voc_scales, aim, cw1, sw, dhid, base, offs):
    idx = unstriped8(offs)
    vocu = unpack_weight(voc_words, voc_scales, "e2m1")
    hidq = mxq(f64(hid), 0, "e4m3")
    a = hidq.T @ vocu
    dhidq = mxq(f64(dhid), 0, "e4m3")
    ta = dhidq.T @ vocu
    m1 = np.max(a, axis=1, keepdims=True)
    p = np.exp(a - m1)
    z = np.sum(p, axis=1, keepdims=True)
    px = np.exp(pick8(a, idx, 16) - m1)
    pm = np.sum(px * f64(cw1), axis=1, keepdims=True)
    u1 = px / pm
    du1 = f64(sw) * u1 * 2.0
    dpm = 4.0 * (pm / z - f64(aim)) * 2.0 / z + np.sum(du1 * px / np.square(pm) * (-1.0), axis=1, keepdims=True)
    dpx = du1 / pm + dpm * f64(cw1)
    dz = 4.0 * (pm / z - f64(aim)) * 2.0 * pm / np.square(z) * (-1.0)
    xp = ta * p
    xz = np.sum(xp, axis=1, keepdims=True)
    xpx = pick8(ta, idx, 16) * px
    xpm = np.sum(xpx * f64(cw1), axis=1, keepdims=True)
    xu1 = (xpx - xpm * px / pm) / pm
    xdu1 = xu1 * f64(sw) * 2.0
    xdpm = ((xpm - xz * pm / z) / z * 4.0 * 2.0 - xz * 4.0 * (pm / z - f64(aim)) * 2.0 / z) / z + np.sum((xdu1 * px + xpx * du1 - xpm * pm * 2.0 * du1 * px / np.square(pm)) / np.square(pm) * (-1.0), axis=1, keepdims=True)
    xdpx = (xdu1 - xpm * du1 / pm) / pm + xdpm * f64(cw1)
    xdz = ((xpm - xz * pm / z) / z * 4.0 * 2.0 * pm + xpm * 4.0 * (pm / z - f64(aim)) * 2.0 - xz * z * 2.0 * 4.0 * (pm / z - f64(aim)) * 2.0 * pm / np.square(z)) / np.square(z) * (-1.0)
    xe1 = xdpx * px + xpx * dpx
    xs1 = np.zeros((Q, V))
    xs1[np.arange(Q)[:, None], idx[np.arange(Q) % 128 // 16]] = xe1
    xda = xdz * p + xp * dz + xs1
    y = xda * 256.0 + f64(base)
    return y

@@ -1,0 +1,259 @@
+from contextlib import ExitStack
+
+import concourse.mybir as mybir
+from concourse.masks import make_identity
+
+D, V, Q, I = 512, 2048, 128, 512
+FLOPS = 2 * 2 * D * V * Q
+
+F32 = mybir.dt.float32
+BF16 = mybir.dt.bfloat16
+I32 = mybir.dt.int32
+U32 = mybir.dt.uint32
+U16 = mybir.dt.uint16
+U8 = mybir.dt.uint8
+FP8X4 = mybir.dt.float8_e4m3fn_x4
+FP4X4 = mybir.dt.float4_e2m1fn_x4
+ALU = mybir.AluOpType
+ACT = mybir.ActivationFunctionType
+AX = mybir.AxisListType
+
+P = 128
+PACK = 4
+N = 512
+NB = V // N
+HALF = 0
+EARLY = 384
+
+
+def tile_attend_hvcoverage_heads_kernel(tc, hid, voc_words, voc_scales, aim, cw1, sw, dhid, base, offs, out):
+    nc = tc.nc
+    mult, add, sub = ALU.mult, ALU.add, ALU.subtract
+    with ExitStack() as ctx:
+        sb = ctx.enter_context(tc.tile_pool(name="sb", bufs=1))
+        ps = ctx.enter_context(tc.psum_pool(name="ps", bufs=1))
+
+        def col(name, n=1):
+            return sb.tile([P, n], F32, name=name)
+
+        def cols(j):
+            return slice(j * N, (j + 1) * N)
+
+        planes = sb.tile([P, V], U8, name="planes", align_bytes=64)
+        nc.gpsimd.memset(planes[:].bitcast(I32), 0)
+        hid_raw = sb.tile([P, PACK, Q], F32, name="hid_raw", tag="hid_then_base")
+        nc.sync.dma_start(out=hid_raw[:], in_=hid.rearrange("(p j) q -> p j q", j=PACK))
+        dhid_raw = sb.tile([P, PACK, Q], F32, name="dhid_raw")
+        nc.scalar.dma_start(out=dhid_raw[:], in_=dhid.rearrange("(p j) q -> p j q", j=PACK))
+        for g in range(4):
+            nc.sync.dma_start(
+                out=planes[32 * g : 32 * g + 4, :].bitcast(I32),
+                in_=voc_scales[0, 4 * g : 4 * g + 4, :].bitcast(I32),
+            )
+        words = []
+        for lo, hi in ((0, 1), (1, NB)):
+            piece = sb.tile([P, 2 * N * (hi - lo)], U8, name="words%d" % lo, align_bytes=64)
+            nc.sync.dma_start(out=piece[:].bitcast(I32), in_=voc_words[0, :, 2 * N * lo : 2 * N * hi].bitcast(I32))
+            words.extend(piece[:, 2 * N * k : 2 * N * (k + 1)] for k in range(hi - lo))
+        offsets = sb.tile([P, I // 16], U16, name="offsets")
+        nc.sync.dma_start(offsets[:], offs)
+        c_col = col("c_col", 4)
+        s_col = col("s_col", 4)
+        aim_col = col("aim_col")
+        nc.sync.dma_start(out=c_col[:], in_=cw1.rearrange("o (p j) -> p (o j)", j=4))
+        nc.sync.dma_start(out=s_col[:], in_=sw.rearrange("o (p j) -> p (o j)", j=4))
+        nc.sync.dma_start(out=aim_col[:], in_=aim)
+
+        warm_in = col("warm_in")
+        warm_out = col("warm_out")
+        nc.gpsimd.memset(warm_in[:], 0.0)
+        nc.scalar.activation(warm_out[:], warm_in[:], ACT.Exp)
+        ident = sb.tile([P, P], F32, name="ident")
+        make_identity(nc, ident[:])
+        of_w = col("of_w", 5)
+        of_aim = col("of_aim", 5)
+        for j, (kw, ka) in enumerate(((-3.0, 2.0), (1.0, -1.0), (-2.0, 1.0), (-1.0, 0.0), (-2048.0, 0.0))):
+            nc.gpsimd.memset(of_w[:, j : j + 1], kw)
+            nc.gpsimd.memset(of_aim[:, j : j + 1], ka)
+        aim5 = col("aim5", 5)
+        nc.gpsimd.tensor_scalar(aim5[:], of_aim[:], aim_col[:], 1.0, mult, mult)
+        zero_q3 = col("zero_q3", 2)
+        nc.gpsimd.memset(zero_q3[:, 0:1], 0.0)
+        xs = sb.tile([P, V], F32, name="xs")
+        nc.vector.memset(xs[:], 0.0)
+
+        hid_bf = sb.tile([P, Q, PACK], BF16, name="hid_bf", align_bytes=64)
+        nc.vector.tensor_copy(out=hid_bf[:], in_=hid_raw[:].rearrange("p j q -> p q j"))
+        dhid_bf = sb.tile([P, Q, PACK], BF16, name="dhid_bf", align_bytes=64)
+        nc.scalar.copy(out=dhid_bf[:], in_=dhid_raw[:].rearrange("p j q -> p q j"))
+        quant = []
+        for name, src in (("hid", hid_bf), ("dhid", dhid_bf)):
+            codes = sb.tile([P, Q], U32, name=name + "_codes", align_bytes=64)
+            scales = sb.tile([P, Q], U8, name=name + "_scales", align_bytes=64)
+            nc.vector.quantize_mx(out=codes[:].bitcast(FP8X4), scales=scales[:], in_=src[:].rearrange("p q j -> p (q j)"))
+            quant.append((codes, scales))
+        base_sb = sb.tile([P, V], F32, name="base_sb", tag="hid_then_base")
+        nc.sync.dma_start(out=base_sb[:], in_=base)
+
+        def product(which, j):
+            codes, scales = quant[which]
+            bank = ps.tile([P, N], F32, name="prod%d_%d" % (which, j), tag="bank%d" % (0 if j == 0 else which * NB + j))
+            nc.tensor.matmul_mx(
+                out=bank[:],
+                lhsT=codes[:].bitcast(FP8X4),
+                lhsT_scale=scales[:],
+                rhs=words[j].bitcast(FP4X4),
+                rhs_scale=planes[:, cols(j)],
+                start=True,
+                stop=True,
+            )
+            return bank
+
+        a_sb = sb.tile([P, V], F32, name="a_sb")
+        ta_sb = sb.tile([P, V], F32, name="ta_sb")
+        part_max = col("part_max", NB)
+        ta_ps = []
+        for j in range(NB):
+            if j == NB - 1:
+                ta_ps.append(product(1, 0))
+            a_ps = product(0, j)
+            nc.vector.tensor_scalar(a_sb[:, cols(j)], a_ps[:], 1.0, None, mult, ALU.max, accum_out=part_max[:, j : j + 1])
+        ta_ps.extend(product(1, j) for j in range(1, NB))
+        neg_m = col("neg_m")
+        nc.vector.tensor_reduce(neg_m[:], part_max[:], AX.X, ALU.max, negate=True)
+        neg_2m = col("neg_2m")
+        nc.gpsimd.tensor_scalar(neg_2m[:], neg_m[:], 2.0, 1.0, mult, mult)
+        p_sb = sb.tile([P, V], F32, name="p_sb")
+        ax = p_sb[:, V - I : V]
+        nc.vector.tensor_copy(ax, a_sb[:].indirect(offsets[:]))
+        for j in range(NB):
+            nc.scalar.copy(out=ta_sb[:, cols(j)], in_=ta_ps[j][:])
+
+        rows = []
+        for k, src in enumerate((c_col, s_col)):
+            bank = ps.tile([P, 4, P], F32, name="row%d" % k, tag="bank%d" % (k + 1))
+            for j in range(4):
+                nc.tensor.transpose(bank[:, j, :], src[:, j : j + 1].to_broadcast([P, P]), ident[:])
+            rows.append(bank[:].rearrange("p j n -> p n j"))
+        c_row, s_row = rows
+
+        def slots(t):
+            return t[:].rearrange("p (n j) -> p n j", j=4)
+
+        part_z = col("part_z", 2)
+        nc.scalar.activation(p_sb[:, :EARLY], a_sb[:, :EARLY], ACT.Exp, bias=neg_m[:], accum_out=part_z[:, 0:1])
+        px = sb.tile([P, I], F32, name="px")
+        nc.scalar.activation(px[:], ax, ACT.Exp, bias=neg_m[:])
+        px2 = sb.tile([P, I], F32, name="px2")
+        nc.scalar.activation(px2[:], ax, ACT.Exp, bias=neg_2m[:], scale=2.0)
+        z = col("z")
+        nc.scalar.activation(p_sb[:, EARLY:], a_sb[:, EARLY:], ACT.Exp, bias=neg_m[:], accum_out=part_z[:, 1:2])
+        nc.scalar.activation(z[:], part_z[:, 0:1], ACT.Identity, bias=part_z[:, 1:2])
+        tx = sb.tile([P, I], F32, name="tx")
+        nc.vector.tensor_copy(tx[:], ta_sb[:].indirect(offsets[:]))
+
+        cp = sb.tile([P, I], F32, name="cp")
+        cpt = sb.tile([P, I], F32, name="cpt")
+        sp2 = sb.tile([P, I], F32, name="sp2")
+        h1 = sb.tile([P, I], F32, name="h1")
+        pm, xpm, r, neg_mu = col("pm"), col("xpm"), col("r"), col("neg_mu")
+        s1, s3, q1 = col("s1"), col("s3"), col("q1")
+        pm5, k1 = col("pm5", 5), col("k1")
+        xp = sb.tile([P, V], F32, name="xp")
+        part_xz = col("part_xz", NB)
+        iz, e5, tab = col("iz"), col("e5", 5), col("tab", 8)
+        ab0 = col("ab0", 2)
+
+        def dense_product(j):
+            nc.vector.scalar_tensor_tensor(
+                xp[:, cols(j)], ta_ps[j][:], iz[:], p_sb[:, cols(j)], mult, mult, accum_out=part_xz[:, j : j + 1]
+            )
+
+        nc.vector.scalar_tensor_tensor(slots(cp), slots(px), 1.0, c_row, mult, mult, accum_out=pm[:])
+        nc.vector.scalar_tensor_tensor(slots(sp2), slots(px2), 1.0, s_row, mult, mult, accum_out=s1[:])
+        nc.vector.reciprocal(r[:], pm[:])
+        nc.vector.scalar_tensor_tensor(cpt[:], cp[:], 1.0, tx[:], mult, mult, accum_out=xpm[:])
+        nc.gpsimd.tensor_scalar(pm5[:], of_w[:], pm[:], 1.0, mult, mult)
+        nc.gpsimd.tensor_scalar(q1[:], s1[:], r[:], -0.5, mult, mult)
+        nc.gpsimd.tensor_scalar(neg_mu[:], xpm[:], r[:], -1.0, mult, mult)
+        nc.gpsimd.tensor_scalar(k1[:], r[:], r[:], 1024.0, mult, mult)
+        nc.vector.reciprocal(iz[:], z[:])
+        gap, wk, beta = col("gap"), col("wk"), col("beta")
+        nc.scalar.activation(gap[:], pm[:], ACT.Identity, scale=iz[:], bias=aim5[:, 1:2])
+        nc.scalar.activation(wk[:], pm5[:, 4:5], ACT.Copy, scale=iz[:])
+        nc.scalar.activation(beta[:], gap[:], ACT.Copy, scale=wk[:])
+        nc.vector.scalar_tensor_tensor(h1[:], tx[:], neg_mu[:], sp2[:], add, mult, accum_out=s3[:])
+        nc.gpsimd.tensor_scalar(zero_q3[:, 1:2], s3[:], r[:], -1.0, mult, mult)
+        dense_product(0)
+        nc.vector.scalar_tensor_tensor(e5[:], pm5[:], iz[:], aim5[:], mult, add)
+        dense_product(1)
+        nc.vector.tensor_scalar(tab[:, 0:3:2], e5[:, 0:3:2], e5[:, 4:5], iz[:], mult, mult)
+        nc.vector.tensor_scalar(tab[:, 3:6], e5[:, 1:4], e5[:, 3:4], pm5[:, 2:3], mult, mult)
+        dense_product(2)
+        nc.vector.tensor_scalar(tab[:, 6:8], tab[:, 3:6:2], q1[:], None, add)
+        dense_product(3)
+        nc.vector.scalar_tensor_tensor(ab0[:], tab[:, 2:8:5], neg_mu[:], zero_q3[:], mult, add)
+        h2a = sb.tile([P, I], F32, name="h2a")
+        h2b = sb.tile([P, I], F32, name="h2b")
+        nc.vector.scalar_tensor_tensor(h2a[:], cpt[:], tab[:, 6:7], h1[:], mult, add)
+        k3, alpha = col("k3"), col("alpha")
+        junk_k, junk_a = col("junk_k", NB), col("junk_a", NB)
+        nc.vector.tensor_scalar(junk_k[:], part_xz[:], tab[:, 4:5], ab0[:, 1:2], mult, add, accum_out=k3[:])
+        nc.vector.tensor_scalar(junk_a[:], part_xz[:], tab[:, 0:1], ab0[:, 0:1], mult, add, accum_out=alpha[:])
+
+        turned = [ps.tile([P, 4, P], F32, name="turned%d" % j, tag="bank%d" % (4, 3, 1, 2)[j]) for j in range(NB)]
+
+        def turn_add(j, src, first, last):
+            for k in range(4):
+                nc.tensor.matmul(
+                    turned[j][:, k, :],
+                    lhsT=src[:, k * P : (k + 1) * P],
+                    rhs=ident[:],
+                    is_transpose=True,
+                    start=first and k == 0,
+                    stop=last and k == 3,
+                )
+
+        back = {}
+
+        def turn_back(j):
+            staged = sb.tile([P, 4, P], F32, name="staged%d" % j)
+            nc.scalar.copy(out=staged[:], in_=turned[j][:])
+            back[j] = ps.tile([P, N], F32, name="back%d" % j, tag="bank%d" % (0 if j == 0 else NB + j))
+            for k in range(4):
+                nc.tensor.transpose(back[j][:, k * P : (k + 1) * P], staged[:, k, :], ident[:])
+
+        def scaled(name, src, j, factor):
+            t = sb.tile([P, N], F32, name="%s%d" % (name, j))
+            nc.scalar.activation(t[:], src[:, cols(j)], ACT.Copy, scale=factor)
+            return t
+
+        for j in range(NB):
+            turn_add(j, base_sb[:, cols(j)], True, False)
+        for j in range(NB):
+            turn_add(j, scaled("bx", xp, j, beta[:]), False, j < HALF)
+
+        nc.vector.tensor_scalar(h2b[:], cp[:], k3[:], None, mult)
+        nc.vector.tensor_tensor(xs[:].indirect(offsets[:]), h2a[:], h2b[:], add)
+
+        for j in range(HALF):
+            turn_back(j)
+        for j in range(HALF, NB):
+            turn_add(j, scaled("ap", p_sb, j, alpha[:]), False, True)
+            if j > HALF:
+                turn_back(j - 1)
+        turn_back(NB - 1)
+
+        for j in range(NB):
+            y = sb.tile([P, N], F32, name="y%d" % j)
+            if j < HALF:
+                y2 = sb.tile([P, N], F32, name="y2_%d" % j)
+                nc.vector.scalar_tensor_tensor(y2[:], p_sb[:, cols(j)], alpha[:], back[j][:], mult, add)
+                nc.vector.scalar_tensor_tensor(y[:], xs[:, cols(j)], k1[:], y2[:], mult, add)
+                nc.sync.dma_start(out=out[:, cols(j)], in_=y[:])
+            else:
+                cuts = (0, N) if j < NB - 1 else (0, N - P, N)
+                for lo, hi in zip(cuts, cuts[1:]):
+                    wide = slice(j * N + lo, j * N + hi)
+                    nc.vector.scalar_tensor_tensor(y[:, lo:hi], xs[:, wide], k1[:], back[j][:, lo:hi], mult, add)
+                    nc.sync.dma_start(out=out[:, wide], in_=y[:, lo:hi])

@@ -22,7 +22,7 @@ P = 128
 PACK = 4
 N = 512
 NB = V // N
-HALF = 0
+HALF = 1
 EARLY = 384
 
 
@@ -40,11 +40,11 @@ def tile_attend_hvcoverage_heads_kernel(tc, hid, voc_words, voc_scales, aim, cw1
             return slice(j * N, (j + 1) * N)
 
         planes = sb.tile([P, V], U8, name="planes", align_bytes=64)
-        nc.gpsimd.memset(planes[:].bitcast(I32), 0)
+        nc.vector.memset(planes[:].bitcast(I32), 0)
         hid_raw = sb.tile([P, PACK, Q], F32, name="hid_raw", tag="hid_then_base")
         nc.sync.dma_start(out=hid_raw[:], in_=hid.rearrange("(p j) q -> p j q", j=PACK))
         dhid_raw = sb.tile([P, PACK, Q], F32, name="dhid_raw")
-        nc.scalar.dma_start(out=dhid_raw[:], in_=dhid.rearrange("(p j) q -> p j q", j=PACK))
+        nc.sync.dma_start(out=dhid_raw[:], in_=dhid.rearrange("(p j) q -> p j q", j=PACK))
         for g in range(4):
             nc.sync.dma_start(
                 out=planes[32 * g : 32 * g + 4, :].bitcast(I32),
@@ -73,18 +73,19 @@ def tile_attend_hvcoverage_heads_kernel(tc, hid, voc_words, voc_scales, aim, cw1
         of_w = col("of_w", 5)
         of_aim = col("of_aim", 5)
         for j, (kw, ka) in enumerate(((-3.0, 2.0), (1.0, -1.0), (-2.0, 1.0), (-1.0, 0.0), (-2048.0, 0.0))):
-            nc.gpsimd.memset(of_w[:, j : j + 1], kw)
-            nc.gpsimd.memset(of_aim[:, j : j + 1], ka)
+            nc.vector.memset(of_w[:, j : j + 1], kw)
+            nc.vector.memset(of_aim[:, j : j + 1], ka)
+        of_r = col("of_r", 2)
+        nc.vector.memset(of_r[:, 0:1], -0.5)
+        nc.vector.memset(of_r[:, 1:2], -1.0)
         aim5 = col("aim5", 5)
-        nc.gpsimd.tensor_scalar(aim5[:], of_aim[:], aim_col[:], 1.0, mult, mult)
+        nc.scalar.activation(aim5[:], of_aim[:], ACT.Copy, scale=aim_col[:])
         zero_q3 = col("zero_q3", 2)
-        nc.gpsimd.memset(zero_q3[:, 0:1], 0.0)
-        xs = sb.tile([P, V], F32, name="xs")
-        nc.vector.memset(xs[:], 0.0)
+        nc.vector.memset(zero_q3[:, 0:1], 0.0)
 
         hid_bf = sb.tile([P, Q, PACK], BF16, name="hid_bf", align_bytes=64)
         nc.vector.tensor_copy(out=hid_bf[:], in_=hid_raw[:].rearrange("p j q -> p q j"))
-        dhid_bf = sb.tile([P, Q, PACK], BF16, name="dhid_bf", align_bytes=64)
+        dhid_bf = sb.tile([P, Q, PACK], BF16, name="dhid_bf", tag="dhid_then_xs", align_bytes=64)
         nc.scalar.copy(out=dhid_bf[:], in_=dhid_raw[:].rearrange("p j q -> p q j"))
         quant = []
         for name, src in (("hid", hid_bf), ("dhid", dhid_bf)):
@@ -92,6 +93,8 @@ def tile_attend_hvcoverage_heads_kernel(tc, hid, voc_words, voc_scales, aim, cw1
             scales = sb.tile([P, Q], U8, name=name + "_scales", align_bytes=64)
             nc.vector.quantize_mx(out=codes[:].bitcast(FP8X4), scales=scales[:], in_=src[:].rearrange("p q j -> p (q j)"))
             quant.append((codes, scales))
+        xs = sb.tile([P, V], F32, name="xs", tag="dhid_then_xs", align_bytes=64)
+        nc.gpsimd.memset(xs[:], 0.0)
         base_sb = sb.tile([P, V], F32, name="base_sb", tag="hid_then_base")
         nc.sync.dma_start(out=base_sb[:], in_=base)
 
@@ -122,7 +125,7 @@ def tile_attend_hvcoverage_heads_kernel(tc, hid, voc_words, voc_scales, aim, cw1
         neg_m = col("neg_m")
         nc.vector.tensor_reduce(neg_m[:], part_max[:], AX.X, ALU.max, negate=True)
         neg_2m = col("neg_2m")
-        nc.gpsimd.tensor_scalar(neg_2m[:], neg_m[:], 2.0, 1.0, mult, mult)
+        nc.scalar.activation(neg_2m[:], neg_m[:], ACT.Copy, scale=2.0)
         p_sb = sb.tile([P, V], F32, name="p_sb")
         ax = p_sb[:, V - I : V]
         nc.vector.tensor_copy(ax, a_sb[:].indirect(offsets[:]))
@@ -173,18 +176,19 @@ def tile_attend_hvcoverage_heads_kernel(tc, hid, voc_words, voc_scales, aim, cw1
         nc.vector.scalar_tensor_tensor(slots(sp2), slots(px2), 1.0, s_row, mult, mult, accum_out=s1[:])
         nc.vector.reciprocal(r[:], pm[:])
         nc.vector.scalar_tensor_tensor(cpt[:], cp[:], 1.0, tx[:], mult, mult, accum_out=xpm[:])
-        nc.gpsimd.tensor_scalar(pm5[:], of_w[:], pm[:], 1.0, mult, mult)
-        nc.gpsimd.tensor_scalar(q1[:], s1[:], r[:], -0.5, mult, mult)
-        nc.gpsimd.tensor_scalar(neg_mu[:], xpm[:], r[:], -1.0, mult, mult)
-        nc.gpsimd.tensor_scalar(k1[:], r[:], r[:], 1024.0, mult, mult)
         nc.vector.reciprocal(iz[:], z[:])
-        gap, wk, beta = col("gap"), col("wk"), col("beta")
+        nc.vector.tensor_scalar(neg_mu[:], xpm[:], r[:], -1.0, mult, mult)
+        gap, wk, beta, r2 = col("gap"), col("wk"), col("beta"), col("r2", 2)
+        nc.scalar.activation(pm5[:], of_w[:], ACT.Copy, scale=pm[:])
         nc.scalar.activation(gap[:], pm[:], ACT.Identity, scale=iz[:], bias=aim5[:, 1:2])
         nc.scalar.activation(wk[:], pm5[:, 4:5], ACT.Copy, scale=iz[:])
         nc.scalar.activation(beta[:], gap[:], ACT.Copy, scale=wk[:])
-        nc.vector.scalar_tensor_tensor(h1[:], tx[:], neg_mu[:], sp2[:], add, mult, accum_out=s3[:])
-        nc.gpsimd.tensor_scalar(zero_q3[:, 1:2], s3[:], r[:], -1.0, mult, mult)
+        nc.scalar.activation(r2[:], of_r[:], ACT.Copy, scale=r[:])
+        nc.scalar.activation(q1[:], s1[:], ACT.Copy, scale=r2[:, 0:1])
+        nc.scalar.activation(k1[:], r[:], ACT.Square, scale=32.0)
         dense_product(0)
+        nc.vector.scalar_tensor_tensor(h1[:], tx[:], neg_mu[:], sp2[:], add, mult, accum_out=s3[:])
+        nc.scalar.activation(zero_q3[:, 1:2], s3[:], ACT.Copy, scale=r2[:, 1:2])
         nc.vector.scalar_tensor_tensor(e5[:], pm5[:], iz[:], aim5[:], mult, add)
         dense_product(1)
         nc.vector.tensor_scalar(tab[:, 0:3:2], e5[:, 0:3:2], e5[:, 4:5], iz[:], mult, mult)

@@ -22,7 +22,7 @@ P = 128
 PACK = 4
 N = 512
 NB = V // N
-HALF = 1
+HALF = 0
 EARLY = 384
 
 
@@ -40,7 +40,7 @@ def tile_attend_hvcoverage_heads_kernel(tc, hid, voc_words, voc_scales, aim, cw1
             return slice(j * N, (j + 1) * N)
 
         planes = sb.tile([P, V], U8, name="planes", align_bytes=64)
-        nc.vector.memset(planes[:].bitcast(I32), 0)
+        nc.gpsimd.memset(planes[:].bitcast(I32), 0)
         hid_raw = sb.tile([P, PACK, Q], F32, name="hid_raw", tag="hid_then_base")
         nc.sync.dma_start(out=hid_raw[:], in_=hid.rearrange("(p j) q -> p j q", j=PACK))
         dhid_raw = sb.tile([P, PACK, Q], F32, name="dhid_raw")
@@ -73,15 +73,15 @@ def tile_attend_hvcoverage_heads_kernel(tc, hid, voc_words, voc_scales, aim, cw1
         of_w = col("of_w", 5)
         of_aim = col("of_aim", 5)
         for j, (kw, ka) in enumerate(((-3.0, 2.0), (1.0, -1.0), (-2.0, 1.0), (-1.0, 0.0), (-2048.0, 0.0))):
-            nc.vector.memset(of_w[:, j : j + 1], kw)
-            nc.vector.memset(of_aim[:, j : j + 1], ka)
+            nc.gpsimd.memset(of_w[:, j : j + 1], kw)
+            nc.gpsimd.memset(of_aim[:, j : j + 1], ka)
         of_r = col("of_r", 2)
-        nc.vector.memset(of_r[:, 0:1], -0.5)
-        nc.vector.memset(of_r[:, 1:2], -1.0)
+        nc.gpsimd.memset(of_r[:, 0:1], -0.5)
+        nc.gpsimd.memset(of_r[:, 1:2], -1.0)
         aim5 = col("aim5", 5)
         nc.scalar.activation(aim5[:], of_aim[:], ACT.Copy, scale=aim_col[:])
         zero_q3 = col("zero_q3", 2)
-        nc.vector.memset(zero_q3[:, 0:1], 0.0)
+        nc.gpsimd.memset(zero_q3[:, 0:1], 0.0)
 
         hid_bf = sb.tile([P, Q, PACK], BF16, name="hid_bf", align_bytes=64)
         nc.vector.tensor_copy(out=hid_bf[:], in_=hid_raw[:].rearrange("p j q -> p q j"))

from contextlib import ExitStack

import concourse.mybir as mybir
from concourse.masks import make_identity

D, V, Q, I = 512, 2048, 128, 512
FLOPS = 2 * 2 * D * V * Q

F32 = mybir.dt.float32
BF16 = mybir.dt.bfloat16
I32 = mybir.dt.int32
U32 = mybir.dt.uint32
U16 = mybir.dt.uint16
U8 = mybir.dt.uint8
FP8X4 = mybir.dt.float8_e4m3fn_x4
FP4X4 = mybir.dt.float4_e2m1fn_x4
ALU = mybir.AluOpType
ACT = mybir.ActivationFunctionType
AX = mybir.AxisListType

P = 128
PACK = 4
N = 512
NB = V // N
HALF = 0
EARLY = 384


def tile_attend_hvcoverage_heads_kernel(tc, hid, voc_words, voc_scales, aim, cw1, sw, dhid, base, offs, out):
    nc = tc.nc
    mult, add, sub = ALU.mult, ALU.add, ALU.subtract
    with ExitStack() as ctx:
        sb = ctx.enter_context(tc.tile_pool(name="sb", bufs=1))
        ps = ctx.enter_context(tc.psum_pool(name="ps", bufs=1))

        def col(name, n=1):
            return sb.tile([P, n], F32, name=name)

        def cols(j):
            return slice(j * N, (j + 1) * N)

        planes = sb.tile([P, V], U8, name="planes", align_bytes=64)
        nc.gpsimd.memset(planes[:].bitcast(I32), 0)
        hid_raw = sb.tile([P, PACK, Q], F32, name="hid_raw", tag="hid_then_base")
        nc.sync.dma_start(out=hid_raw[:], in_=hid.rearrange("(p j) q -> p j q", j=PACK))
        dhid_raw = sb.tile([P, PACK, Q], F32, name="dhid_raw")
        nc.sync.dma_start(out=dhid_raw[:], in_=dhid.rearrange("(p j) q -> p j q", j=PACK))
        for g in range(4):
            nc.sync.dma_start(
                out=planes[32 * g : 32 * g + 4, :].bitcast(I32),
                in_=voc_scales[0, 4 * g : 4 * g + 4, :].bitcast(I32),
            )
        words = []
        for lo, hi in ((0, 1), (1, NB)):
            piece = sb.tile([P, 2 * N * (hi - lo)], U8, name="words%d" % lo, align_bytes=64)
            nc.sync.dma_start(out=piece[:].bitcast(I32), in_=voc_words[0, :, 2 * N * lo : 2 * N * hi].bitcast(I32))
            words.extend(piece[:, 2 * N * k : 2 * N * (k + 1)] for k in range(hi - lo))
        offsets = sb.tile([P, I // 16], U16, name="offsets")
        nc.sync.dma_start(offsets[:], offs)
        c_col = col("c_col", 4)
        s_col = col("s_col", 4)
        aim_col = col("aim_col")
        nc.sync.dma_start(out=c_col[:], in_=cw1.rearrange("o (p j) -> p (o j)", j=4))
        nc.sync.dma_start(out=s_col[:], in_=sw.rearrange("o (p j) -> p (o j)", j=4))
        nc.sync.dma_start(out=aim_col[:], in_=aim)

        warm_in = col("warm_in")
        warm_out = col("warm_out")
        nc.gpsimd.memset(warm_in[:], 0.0)
        nc.scalar.activation(warm_out[:], warm_in[:], ACT.Exp)
        ident = sb.tile([P, P], F32, name="ident")
        make_identity(nc, ident[:])
        of_w = col("of_w", 5)
        of_aim = col("of_aim", 5)
        for j, (kw, ka) in enumerate(((-3.0, 2.0), (1.0, -1.0), (-2.0, 1.0), (-1.0, 0.0), (-2048.0, 0.0))):
            nc.gpsimd.memset(of_w[:, j : j + 1], kw)
            nc.gpsimd.memset(of_aim[:, j : j + 1], ka)
        of_r = col("of_r", 2)
        nc.gpsimd.memset(of_r[:, 0:1], -0.5)
        nc.gpsimd.memset(of_r[:, 1:2], -1.0)
        aim5 = col("aim5", 5)
        nc.scalar.activation(aim5[:], of_aim[:], ACT.Copy, scale=aim_col[:])
        zero_q3 = col("zero_q3", 2)
        nc.gpsimd.memset(zero_q3[:, 0:1], 0.0)

        hid_bf = sb.tile([P, Q, PACK], BF16, name="hid_bf", align_bytes=64)
        nc.vector.tensor_copy(out=hid_bf[:], in_=hid_raw[:].rearrange("p j q -> p q j"))
        dhid_bf = sb.tile([P, Q, PACK], BF16, name="dhid_bf", tag="dhid_then_xs", align_bytes=64)
        nc.scalar.copy(out=dhid_bf[:], in_=dhid_raw[:].rearrange("p j q -> p q j"))
        quant = []
        for name, src in (("hid", hid_bf), ("dhid", dhid_bf)):
            codes = sb.tile([P, Q], U32, name=name + "_codes", align_bytes=64)
            scales = sb.tile([P, Q], U8, name=name + "_scales", align_bytes=64)
            nc.vector.quantize_mx(out=codes[:].bitcast(FP8X4), scales=scales[:], in_=src[:].rearrange("p q j -> p (q j)"))
            quant.append((codes, scales))
        xs = sb.tile([P, V], F32, name="xs", tag="dhid_then_xs", align_bytes=64)
        nc.gpsimd.memset(xs[:], 0.0)
        base_sb = sb.tile([P, V], F32, name="base_sb", tag="hid_then_base")
        nc.sync.dma_start(out=base_sb[:], in_=base)

        def product(which, j):
            codes, scales = quant[which]
            bank = ps.tile([P, N], F32, name="prod%d_%d" % (which, j), tag="bank%d" % (0 if j == 0 else which * NB + j))
            nc.tensor.matmul_mx(
                out=bank[:],
                lhsT=codes[:].bitcast(FP8X4),
                lhsT_scale=scales[:],
                rhs=words[j].bitcast(FP4X4),
                rhs_scale=planes[:, cols(j)],
                start=True,
                stop=True,
            )
            return bank

        a_sb = sb.tile([P, V], F32, name="a_sb")
        ta_sb = sb.tile([P, V], F32, name="ta_sb")
        part_max = col("part_max", NB)
        ta_ps = []
        for j in range(NB):
            if j == NB - 1:
                ta_ps.append(product(1, 0))
            a_ps = product(0, j)
            nc.vector.tensor_scalar(a_sb[:, cols(j)], a_ps[:], 1.0, None, mult, ALU.max, accum_out=part_max[:, j : j + 1])
        ta_ps.extend(product(1, j) for j in range(1, NB))
        neg_m = col("neg_m")
        nc.vector.tensor_reduce(neg_m[:], part_max[:], AX.X, ALU.max, negate=True)
        neg_2m = col("neg_2m")
        nc.scalar.activation(neg_2m[:], neg_m[:], ACT.Copy, scale=2.0)
        p_sb = sb.tile([P, V], F32, name="p_sb")
        ax = p_sb[:, V - I : V]
        nc.vector.tensor_copy(ax, a_sb[:].indirect(offsets[:]))
        for j in range(NB):
            nc.scalar.copy(out=ta_sb[:, cols(j)], in_=ta_ps[j][:])

        rows = []
        for k, src in enumerate((c_col, s_col)):
            bank = ps.tile([P, 4, P], F32, name="row%d" % k, tag="bank%d" % (k + 1))
            for j in range(4):
                nc.tensor.transpose(bank[:, j, :], src[:, j : j + 1].to_broadcast([P, P]), ident[:])
            rows.append(bank[:].rearrange("p j n -> p n j"))
        c_row, s_row = rows

        def slots(t):
            return t[:].rearrange("p (n j) -> p n j", j=4)

        part_z = col("part_z", 2)
        nc.scalar.activation(p_sb[:, :EARLY], a_sb[:, :EARLY], ACT.Exp, bias=neg_m[:], accum_out=part_z[:, 0:1])
        px = sb.tile([P, I], F32, name="px")
        nc.scalar.activation(px[:], ax, ACT.Exp, bias=neg_m[:])
        px2 = sb.tile([P, I], F32, name="px2")
        nc.scalar.activation(px2[:], ax, ACT.Exp, bias=neg_2m[:], scale=2.0)
        z = col("z")
        nc.scalar.activation(p_sb[:, EARLY:], a_sb[:, EARLY:], ACT.Exp, bias=neg_m[:], accum_out=part_z[:, 1:2])
        nc.scalar.activation(z[:], part_z[:, 0:1], ACT.Identity, bias=part_z[:, 1:2])
        tx = sb.tile([P, I], F32, name="tx")
        nc.vector.tensor_copy(tx[:], ta_sb[:].indirect(offsets[:]))

        cp = sb.tile([P, I], F32, name="cp")
        cpt = sb.tile([P, I], F32, name="cpt")
        sp2 = sb.tile([P, I], F32, name="sp2")
        h1 = sb.tile([P, I], F32, name="h1")
        pm, xpm, r, neg_mu = col("pm"), col("xpm"), col("r"), col("neg_mu")
        s1, s3, q1 = col("s1"), col("s3"), col("q1")
        pm5, k1 = col("pm5", 5), col("k1")
        xp = sb.tile([P, V], F32, name="xp")
        part_xz = col("part_xz", NB)
        iz, e5, tab = col("iz"), col("e5", 5), col("tab", 8)
        ab0 = col("ab0", 2)

        def dense_product(j):
            nc.vector.scalar_tensor_tensor(
                xp[:, cols(j)], ta_ps[j][:], iz[:], p_sb[:, cols(j)], mult, mult, accum_out=part_xz[:, j : j + 1]
            )

        nc.vector.scalar_tensor_tensor(slots(cp), slots(px), 1.0, c_row, mult, mult, accum_out=pm[:])
        nc.vector.scalar_tensor_tensor(slots(sp2), slots(px2), 1.0, s_row, mult, mult, accum_out=s1[:])
        nc.vector.reciprocal(r[:], pm[:])
        nc.vector.scalar_tensor_tensor(cpt[:], cp[:], 1.0, tx[:], mult, mult, accum_out=xpm[:])
        nc.vector.reciprocal(iz[:], z[:])
        nc.vector.tensor_scalar(neg_mu[:], xpm[:], r[:], -1.0, mult, mult)
        gap, wk, beta, r2 = col("gap"), col("wk"), col("beta"), col("r2", 2)
        nc.scalar.activation(pm5[:], of_w[:], ACT.Copy, scale=pm[:])
        nc.scalar.activation(gap[:], pm[:], ACT.Identity, scale=iz[:], bias=aim5[:, 1:2])
        nc.scalar.activation(wk[:], pm5[:, 4:5], ACT.Copy, scale=iz[:])
        nc.scalar.activation(beta[:], gap[:], ACT.Copy, scale=wk[:])
        nc.scalar.activation(r2[:], of_r[:], ACT.Copy, scale=r[:])
        nc.scalar.activation(q1[:], s1[:], ACT.Copy, scale=r2[:, 0:1])
        nc.scalar.activation(k1[:], r[:], ACT.Square, scale=32.0)
        dense_product(0)
        nc.vector.scalar_tensor_tensor(h1[:], tx[:], neg_mu[:], sp2[:], add, mult, accum_out=s3[:])
        nc.scalar.activation(zero_q3[:, 1:2], s3[:], ACT.Copy, scale=r2[:, 1:2])
        nc.vector.scalar_tensor_tensor(e5[:], pm5[:], iz[:], aim5[:], mult, add)
        dense_product(1)
        nc.vector.tensor_scalar(tab[:, 0:3:2], e5[:, 0:3:2], e5[:, 4:5], iz[:], mult, mult)
        nc.vector.tensor_scalar(tab[:, 3:6], e5[:, 1:4], e5[:, 3:4], pm5[:, 2:3], mult, mult)
        dense_product(2)
        nc.vector.tensor_scalar(tab[:, 6:8], tab[:, 3:6:2], q1[:], None, add)
        dense_product(3)
        nc.vector.scalar_tensor_tensor(ab0[:], tab[:, 2:8:5], neg_mu[:], zero_q3[:], mult, add)
        h2a = sb.tile([P, I], F32, name="h2a")
        h2b = sb.tile([P, I], F32, name="h2b")
        nc.vector.scalar_tensor_tensor(h2a[:], cpt[:], tab[:, 6:7], h1[:], mult, add)
        k3, alpha = col("k3"), col("alpha")
        junk_k, junk_a = col("junk_k", NB), col("junk_a", NB)
        nc.vector.tensor_scalar(junk_k[:], part_xz[:], tab[:, 4:5], ab0[:, 1:2], mult, add, accum_out=k3[:])
        nc.vector.tensor_scalar(junk_a[:], part_xz[:], tab[:, 0:1], ab0[:, 0:1], mult, add, accum_out=alpha[:])

        turned = [ps.tile([P, 4, P], F32, name="turned%d" % j, tag="bank%d" % (4, 3, 1, 2)[j]) for j in range(NB)]

        def turn_add(j, src, first, last):
            for k in range(4):
                nc.tensor.matmul(
                    turned[j][:, k, :],
                    lhsT=src[:, k * P : (k + 1) * P],
                    rhs=ident[:],
                    is_transpose=True,
                    start=first and k == 0,
                    stop=last and k == 3,
                )

        back = {}

        def turn_back(j):
            staged = sb.tile([P, 4, P], F32, name="staged%d" % j)
            nc.scalar.copy(out=staged[:], in_=turned[j][:])
            back[j] = ps.tile([P, N], F32, name="back%d" % j, tag="bank%d" % (0 if j == 0 else NB + j))
            for k in range(4):
                nc.tensor.transpose(back[j][:, k * P : (k + 1) * P], staged[:, k, :], ident[:])

        def scaled(name, src, j, factor):
            t = sb.tile([P, N], F32, name="%s%d" % (name, j))
            nc.scalar.activation(t[:], src[:, cols(j)], ACT.Copy, scale=factor)
            return t

        for j in range(NB):
            turn_add(j, base_sb[:, cols(j)], True, False)
        for j in range(NB):
            turn_add(j, scaled("bx", xp, j, beta[:]), False, j < HALF)

        nc.vector.tensor_scalar(h2b[:], cp[:], k3[:], None, mult)
        nc.vector.tensor_tensor(xs[:].indirect(offsets[:]), h2a[:], h2b[:], add)

        for j in range(HALF):
            turn_back(j)
        for j in range(HALF, NB):
            turn_add(j, scaled("ap", p_sb, j, alpha[:]), False, True)
            if j > HALF:
                turn_back(j - 1)
        turn_back(NB - 1)

        for j in range(NB):
            y = sb.tile([P, N], F32, name="y%d" % j)
            if j < HALF:
                y2 = sb.tile([P, N], F32, name="y2_%d" % j)
                nc.vector.scalar_tensor_tensor(y2[:], p_sb[:, cols(j)], alpha[:], back[j][:], mult, add)
                nc.vector.scalar_tensor_tensor(y[:], xs[:, cols(j)], k1[:], y2[:], mult, add)
                nc.sync.dma_start(out=out[:, cols(j)], in_=y[:])
            else:
                cuts = (0, N) if j < NB - 1 else (0, N - P, N)
                for lo, hi in zip(cuts, cuts[1:]):
                    wide = slice(j * N + lo, j * N + hi)
                    nc.vector.scalar_tensor_tensor(y[:, lo:hi], xs[:, wide], k1[:], back[j][:, lo:hi], mult, add)
                    nc.sync.dma_start(out=out[:, wide], in_=y[:, lo:hi])
